import numpy as np, ml_dtypes
CORES = [35,38,43,46]
N = 4
QP = 128
WID = [128,112,128,16]
def setup_inputs(rng):
    return {"q": rng.standard_normal((N, 128, QP), dtype=np.float32).astype(ml_dtypes.bfloat16), "k": rng.standard_normal((N, 128, 128), dtype=np.float32).astype(ml_dtypes.bfloat16), "v": rng.standard_normal((N, 128, 128), dtype=np.float32).astype(ml_dtypes.bfloat16)}
def setup_inputs_big(rng):
    d = setup_inputs(rng)
    for k in ("q", "k", "v"): d[k] = (d[k].astype(np.float32) * 1024.0).astype(d[k].dtype)
    return d
def setup_inputs_small(rng):
    d = setup_inputs(rng)
    for k in ("q", "k", "v"): d[k] = (d[k].astype(np.float32) * (1 / 1024.0)).astype(d[k].dtype)
    return d
def setup_inputs_apart(rng):
    d = setup_inputs(rng)
    f = (10.0 ** rng.permutation(np.linspace(-1.5, 1.5, N))).astype(np.float32).reshape(N, 1, 1)
    for k in ("q", "k", "v"): d[k] = (d[k].astype(np.float32) * f).astype(d[k].dtype)
    return d
def whole(q, k, v):
    Q, K, V = q.astype(np.float64), k.astype(np.float64), v.astype(np.float64)
    y = np.zeros((N, 128, QP))
    for r in range(N):
        S = [K[j].T @ Q[r] for j in range(N)]
        m = np.max([s.max(axis=0) for s in S], axis=0)
        y[r] = sum(V[j].T @ np.maximum(S[j] - 0.5 * m, 0.0) for j in range(N))
    return {"y": y.astype(ml_dtypes.bfloat16)}
def reference(q, k, v):
    o = whole(q, k, v)["y"].copy()
    for r in range(N):
        o[r][:, WID[r]:] = np.nan
    return {"y": o}

@@ -1,0 +1,196 @@
+from concourse.bass import DstId, RemoteDMATransfer
+from concourse.mybir import AluOpType
+
+NR = 4
+D = 128
+SLOT = 2 * D
+
+SCRATCH = {
+    "qs": ("sbuf", [D, D], "bfloat16"),
+    "kv": ("sbuf", [D, NR * SLOT], "bfloat16"),
+    "idsrc": ("sbuf", [D, D + 1], "bfloat16"),
+    "iddram": ("dram", [D + 1, D], "bfloat16"),
+    "negi": ("sbuf", [D, D], "bfloat16"),
+    "ones": ("sbuf", [D, D], "bfloat16"),
+    "zeros": ("sbuf", [D, D], "float32"),
+    "run": ("sbuf", [D, NR * D], "float32"),
+    "tree": ("sbuf", [D, D], "float32"),
+    "mcol": ("sbuf", [D, 8], "bfloat16"),
+    "mrow": ("sbuf", [D, D], "bfloat16"),
+    "pb": ("sbuf", [D, NR * D], "bfloat16"),
+    "ysb": ("sbuf", [D, D], "bfloat16"),
+}
+for _i in range(NR):
+    SCRATCH["pt%d" % _i] = ("psum", [D, 512], "float32")
+    SCRATCH["ps%d" % _i] = ("psum", [D, 512], "float32")
+
+SEMAPHORES = (["kld", "vld", "qld", "ms0", "idm", "id1", "id2", "one", "zer", "sent", "trp", "mrw", "yps", "ycp", "sto"]
+              + ["ka%d" % i for i in range(NR)] + ["va%d" % i for i in range(NR)]
+              + ["st%d" % i for i in range(NR)] + ["ru%d" % i for i in range(NR)]
+              + ["tr%d" % i for i in range(7)]
+              + ["sb%d" % i for i in range(NR)] + ["pp%d" % i for i in range(NR)])
+
+
+def _bits(mask):
+    return [e for e in range(mask.bit_length()) if (mask >> e) & 1]
+
+
+def _pow2(n):
+    p = 1
+    while p * 2 <= n:
+        p *= 2
+    return p
+
+
+def _plan(src, cores, topo):
+    others = [c for c in cores if c != src]
+    far = [c for c in others if topo.chip(c) != topo.chip(src)]
+    near = [c for c in others if topo.chip(c) == topo.chip(src)]
+    plan = {}
+    used = []
+    if far:
+        eng = [e for e in _bits(topo.mask(src, far[0])) if all((topo.mask(src, c) >> e) & 1 for c in far)]
+        n = _pow2(len(eng) // len(far))
+        for i, c in enumerate(far):
+            plan[c] = eng[i * n:(i + 1) * n]
+            used += plan[c]
+    if near:
+        eng = [e for e in _bits(topo.mask(src, near[0])) if e not in used]
+        n = _pow2(len(eng) // len(near))
+        for i, c in enumerate(near):
+            plan[c] = eng[i * n:(i + 1) * n]
+    return far, near, plan
+
+
+def _mask(engines):
+    return sum(1 << e for e in engines)
+
+
+def rank_program(g, core, T, topo):
+    r = T.rank_of(core)
+    if r is None:
+        return
+    cores = list(T.cores)
+    W = T.tables["WID"][r]
+    sem = T.sem
+    pe, ve, sy, sc = g.tensor, g.vector, g.sync, g.scalar
+    far, near, plan = _plan(core, cores, topo)
+    for c in far + near:
+        assert topo.may_write(core, c)
+
+    def kcol(j):
+        return T.kv[:, j * SLOT:j * SLOT + D]
+
+    def vcol(j):
+        return T.kv[:, j * SLOT + D:(j + 1) * SLOT]
+
+    def slot(j):
+        return T.kv[:, j * SLOT:(j + 1) * SLOT]
+
+    sy.dma_start(kcol(r), T.k[:, :]).then_inc(sem.kld, 16)
+    sc.dma_start(vcol(r), T.v[:, :]).then_inc(sem.vld, 16)
+    sy.dma_start(T.qs[:, 0:W], T.q[:, 0:W]).then_inc(sem.qld, 16)
+
+    ve.memset(T.idsrc[:, :], 0.0).then_inc(sem.ms0, 1)
+    ve.wait_ge(sem.ms0, 1)
+    ve.memset(T.idsrc[:, 0:1], -0.5).then_inc(sem.idm, 1)
+    ve.memset(T.ones[0:1, :], 1.0).then_inc(sem.one, 1)
+    ve.memset(T.zeros[:, 0:W], 0.0).then_inc(sem.zer, 1)
+    sc.wait_ge(sem.idm, 1)
+    sc.dma_start(T.iddram[:, :], T.idsrc[:, :]).then_inc(sem.id1, 16)
+    sc.wait_ge(sem.id1, 16)
+    sc.dma_start(T.negi[:, :], T.iddram[0:D, :]).then_inc(sem.id2, 16)
+
+    def xfer(dst_core, ap, rsem):
+        rid, pid, _se = topo.addr(dst_core)
+        return RemoteDMATransfer(dst_ids=[DstId(rid=rid, pnc=pid)], dma_engine_mask=_mask(plan[dst_core]),
+                                 remote_sem=rsem, src=ap, dst=ap)
+
+    sent = 0
+    g.wait_ge(sem.kld, 16)
+    if far:
+        g.remote_dma_fused([xfer(c, kcol(r), sem["ka%d" % r]) for c in far], local_sem=sem.sent)
+        sent += sum(len(plan[c]) for c in far)
+    g.wait_ge(sem.vld, 16)
+    if near:
+        g.remote_dma_fused([xfer(c, slot(r), sem["ka%d" % r]) for c in near], local_sem=sem.sent)
+        sent += sum(len(plan[c]) for c in near)
+    if far:
+        g.remote_dma_fused([xfer(c, vcol(r), sem["va%d" % r]) for c in far], local_sem=sem.sent)
+        sent += sum(len(plan[c]) for c in far)
+
+    order = [r] + [T.rank_of(c) for c in near] + [T.rank_of(c) for c in far]
+    near_ranks = [T.rank_of(c) for c in near]
+
+    def k_wait(j):
+        if j == r:
+            return sem.kld, 16
+        return sem["ka%d" % j], len(_plan(cores[j], cores, topo)[2][core])
+
+    def v_wait(j):
+        if j == r:
+            return sem.vld, 16
+        if j in near_ranks:
+            return k_wait(j)
+        return sem["va%d" % j], len(_plan(cores[j], cores, topo)[2][core])
+
+    YP = T.pt0[:, 256:256 + W]
+    MP = T.pt1[0:1, 256:256 + W]
+
+    pe.wait_ge(sem.qld, 16)
+    for i, j in enumerate(order):
+        s, n = k_wait(j)
+        pe.wait_ge(s, n)
+        pe.matmul(T["pt%d" % i][0:W, 0:D], T.qs[:, 0:W], kcol(j), True, True).then_inc(sem["st%d" % i], 1)
+        pe.matmul(T["ps%d" % i][:, 0:W], kcol(j), T.qs[:, 0:W], True, False)
+
+    for i in range(NR):
+        ve.wait_ge(sem["st%d" % i], 1)
+        out = T.run[0:W, i * D:(i + 1) * D]
+        if i == 0:
+            ve.tensor_copy(out, T.pt0[0:W, 0:D]).then_inc(sem.ru0, 1)
+        else:
+            ve.wait_ge(sem["ru%d" % (i - 1)], 1)
+            ve.tensor_tensor(out, T["pt%d" % i][0:W, 0:D], T.run[0:W, (i - 1) * D:i * D],
+                             AluOpType.max).then_inc(sem["ru%d" % i], 1)
+    buf, o, width, off, lvl = T.run, (NR - 1) * D, D, 0, 0
+    prev = sem["ru%d" % (NR - 1)]
+    while width > 1:
+        h = width // 2
+        out = T.mcol[0:W, 0:1] if h == 1 else T.tree[0:W, off:off + h]
+        ve.wait_ge(prev, 1)
+        ve.tensor_tensor(out, buf[0:W, o:o + h], buf[0:W, o + h:o + width], AluOpType.max).then_inc(sem["tr%d" % lvl], 1)
+        prev = sem["tr%d" % lvl]
+        buf, o, width = T.tree, off, h
+        off += h
+        lvl += 1
+
+    pe.wait_ge(prev, 1)
+    pe.wait_ge(sem.id2, 16)
+    pe.matmul(MP, T.mcol[0:W, 0:1], T.negi[0:W, 0:W], True, True).then_inc(sem.trp, 1)
+    ve.wait_ge(sem.trp, 1)
+    ve.tensor_copy(T.mrow[0:1, 0:W], MP).then_inc(sem.mrw, 1)
+    pe.wait_ge(sem.mrw, 1)
+    pe.wait_ge(sem.one, 1)
+    for i in range(NR):
+        pe.matmul(T["ps%d" % i][:, 0:W], T.ones[0:1, 0:D], T.mrow[0:1, 0:W], False, True).then_inc(sem["sb%d" % i], 1)
+    ve.wait_ge(sem.zer, 1)
+    for i in range(NR):
+        ve.wait_ge(sem["sb%d" % i], 1)
+        ve.tensor_tensor(T.pb[:, i * D:i * D + W], T["ps%d" % i][:, 0:W], T.zeros[:, 0:W],
+                         AluOpType.max).then_inc(sem["pp%d" % i], 1)
+
+    for i, j in enumerate(order):
+        pe.wait_ge(sem["pp%d" % i], 1)
+        s, n = v_wait(j)
+        pe.wait_ge(s, n)
+        mm = pe.matmul(YP, vcol(j), T.pb[:, i * D:i * D + W], i == 0, i == NR - 1)
+        if i == NR - 1:
+            mm.then_inc(sem.yps, 1)
+    ve.wait_ge(sem.yps, 1)
+    ve.tensor_copy(T.ysb[:, 0:W], YP).then_inc(sem.ycp, 1)
+    sy.wait_ge(sem.ycp, 1)
+    sy.dma_start(T.y[:, 0:W], T.ysb[:, 0:W]).then_inc(sem.sto, 16)
+    sy.wait_ge(sem.sto, 16)
+
+    g.wait_ge(sem.sent, sent)

@@ -1,5 +1,5 @@
 from concourse.bass import DstId, RemoteDMATransfer
-from concourse.mybir import AluOpType
+from concourse.mybir import AluOpType, AxisListType
 
 NR = 4
 D = 128
@@ -8,15 +8,13 @@ SLOT = 2 * D
 SCRATCH = {
     "qs": ("sbuf", [D, D], "bfloat16"),
     "kv": ("sbuf", [D, NR * SLOT], "bfloat16"),
-    "idsrc": ("sbuf", [D, D + 1], "bfloat16"),
-    "iddram": ("dram", [D + 1, D], "bfloat16"),
-    "negi": ("sbuf", [D, D], "bfloat16"),
-    "ones": ("sbuf", [D, D], "bfloat16"),
-    "zeros": ("sbuf", [D, D], "float32"),
-    "run": ("sbuf", [D, NR * D], "float32"),
-    "tree": ("sbuf", [D, D], "float32"),
-    "mcol": ("sbuf", [D, 8], "bfloat16"),
-    "mrow": ("sbuf", [D, D], "bfloat16"),
+    "zb": ("sbuf", [D, D], "bfloat16"),
+    "on": ("sbuf", [D, D], "bfloat16"),
+    "zf": ("sbuf", [D, D], "float32"),
+    "cidx": ("sbuf", [D, D], "bfloat16"),
+    "ident": ("sbuf", [D, D], "bfloat16"),
+    "sc": ("sbuf", [D, NR * D], "float32"),
+    "dg": ("sbuf", [D, D], "bfloat16"),
     "pb": ("sbuf", [D, NR * D], "bfloat16"),
     "ysb": ("sbuf", [D, D], "bfloat16"),
 }
@@ -24,10 +22,9 @@ for _i in range(NR):
     SCRATCH["pt%d" % _i] = ("psum", [D, 512], "float32")
     SCRATCH["ps%d" % _i] = ("psum", [D, 512], "float32")
 
-SEMAPHORES = (["kld", "vld", "qld", "ms0", "idm", "id1", "id2", "one", "zer", "sent", "trp", "mrw", "yps", "ycp", "sto"]
+SEMAPHORES = (["kld", "vld", "qld", "ms", "cix", "rix", "idn", "sent", "dgs", "yps", "ycp", "sto"]
               + ["ka%d" % i for i in range(NR)] + ["va%d" % i for i in range(NR)]
               + ["st%d" % i for i in range(NR)] + ["ru%d" % i for i in range(NR)]
-              + ["tr%d" % i for i in range(7)]
               + ["sb%d" % i for i in range(NR)] + ["pp%d" % i for i in range(NR)])
 
 
@@ -91,15 +88,18 @@ def rank_program(g, core, T, topo):
     sc.dma_start(vcol(r), T.v[:, :]).then_inc(sem.vld, 16)
     sy.dma_start(T.qs[:, 0:W], T.q[:, 0:W]).then_inc(sem.qld, 16)
 
-    ve.memset(T.idsrc[:, :], 0.0).then_inc(sem.ms0, 1)
-    ve.wait_ge(sem.ms0, 1)
-    ve.memset(T.idsrc[:, 0:1], -0.5).then_inc(sem.idm, 1)
-    ve.memset(T.ones[0:1, :], 1.0).then_inc(sem.one, 1)
-    ve.memset(T.zeros[:, 0:W], 0.0).then_inc(sem.zer, 1)
-    sc.wait_ge(sem.idm, 1)
-    sc.dma_start(T.iddram[:, :], T.idsrc[:, :]).then_inc(sem.id1, 16)
-    sc.wait_ge(sem.id1, 16)
-    sc.dma_start(T.negi[:, :], T.iddram[0:D, :]).then_inc(sem.id2, 16)
+    RI = T.pt3[:, 256:256 + D]
+    ve.memset(T.zb[:, :], 0.0).then_inc(sem.ms, 1)
+    ve.memset(T.on[:, :], 1.0).then_inc(sem.ms, 1)
+    ve.memset(T.zf[:, :], 0.0).then_inc(sem.ms, 1)
+    ve.wait_ge(sem.ms, 3)
+    ve.tensor_tensor_scan(T.cidx[:, :], T.zb[:, :], T.on[:, :], 0.0, AluOpType.add, AluOpType.add).then_inc(sem.cix, 1)
+    pe.wait_ge(sem.ms, 3)
+    pe.wait_ge(sem.cix, 1)
+    pe.matmul(RI, T.cidx[0:1, :], T.on[0:1, :], True, True).then_inc(sem.rix, 1)
+    ve.wait_ge(sem.cix, 1)
+    ve.wait_ge(sem.rix, 1)
+    ve.tensor_tensor(T.ident[:, :], RI, T.cidx[:, :], AluOpType.is_equal).then_inc(sem.idn, 1)
 
     def xfer(dst_core, ap, rsem):
         rid, pid, _se = topo.addr(dst_core)
@@ -121,6 +121,7 @@ def rank_program(g, core, T, topo):
 
     order = [r] + [T.rank_of(c) for c in near] + [T.rank_of(c) for c in far]
     near_ranks = [T.rank_of(c) for c in near]
+    early = 1 + len(near)
 
     def k_wait(j):
         if j == r:
@@ -135,49 +136,47 @@ def rank_program(g, core, T, topo):
         return sem["va%d" % j], len(_plan(cores[j], cores, topo)[2][core])
 
     YP = T.pt0[:, 256:256 + W]
-    MP = T.pt1[0:1, 256:256 + W]
+
+    def st_mm(i, j):
+        pe.matmul(T["pt%d" % i][0:W, 0:D], T.qs[:, 0:W], kcol(j), True, True).then_inc(sem["st%d" % i], 1)
+
+    def s_mm(i, j):
+        pe.matmul(T["ps%d" % i][:, 0:W], kcol(j), T.qs[:, 0:W], True, False)
 
     pe.wait_ge(sem.qld, 16)
+    pe.wait_ge(sem.idn, 1)
     for i, j in enumerate(order):
         s, n = k_wait(j)
         pe.wait_ge(s, n)
-        pe.matmul(T["pt%d" % i][0:W, 0:D], T.qs[:, 0:W], kcol(j), True, True).then_inc(sem["st%d" % i], 1)
-        pe.matmul(T["ps%d" % i][:, 0:W], kcol(j), T.qs[:, 0:W], True, False)
+        st_mm(i, j)
+        if i < early:
+            s_mm(i, j)
+    for i, j in enumerate(order):
+        if i >= early:
+            s_mm(i, j)
+
+    def mcol(i):
+        return T.sc[0:W, i * D + D - 1:(i + 1) * D]
 
     for i in range(NR):
         ve.wait_ge(sem["st%d" % i], 1)
-        out = T.run[0:W, i * D:(i + 1) * D]
         if i == 0:
-            ve.tensor_copy(out, T.pt0[0:W, 0:D]).then_inc(sem.ru0, 1)
+            ve.tensor_reduce(mcol(0), T.pt0[0:W, 0:D], AxisListType.X, AluOpType.max).then_inc(sem.ru0, 1)
         else:
             ve.wait_ge(sem["ru%d" % (i - 1)], 1)
-            ve.tensor_tensor(out, T["pt%d" % i][0:W, 0:D], T.run[0:W, (i - 1) * D:i * D],
-                             AluOpType.max).then_inc(sem["ru%d" % i], 1)
-    buf, o, width, off, lvl = T.run, (NR - 1) * D, D, 0, 0
-    prev = sem["ru%d" % (NR - 1)]
-    while width > 1:
-        h = width // 2
-        out = T.mcol[0:W, 0:1] if h == 1 else T.tree[0:W, off:off + h]
-        ve.wait_ge(prev, 1)
-        ve.tensor_tensor(out, buf[0:W, o:o + h], buf[0:W, o + h:o + width], AluOpType.max).then_inc(sem["tr%d" % lvl], 1)
-        prev = sem["tr%d" % lvl]
-        buf, o, width = T.tree, off, h
-        off += h
-        lvl += 1
+            ve.tensor_tensor_scan(T.sc[0:W, i * D:(i + 1) * D], T["pt%d" % i][0:W, 0:D], T.zf[0:W, :], mcol(i - 1),
+                                  AluOpType.max, AluOpType.add).then_inc(sem["ru%d" % i], 1)
 
-    pe.wait_ge(prev, 1)
-    pe.wait_ge(sem.id2, 16)
-    pe.matmul(MP, T.mcol[0:W, 0:1], T.negi[0:W, 0:W], True, True).then_inc(sem.trp, 1)
-    ve.wait_ge(sem.trp, 1)
-    ve.tensor_copy(T.mrow[0:1, 0:W], MP).then_inc(sem.mrw, 1)
-    pe.wait_ge(sem.mrw, 1)
-    pe.wait_ge(sem.one, 1)
+    ve.wait_ge(sem["ru%d" % (NR - 1)], 1)
+    ve.wait_ge(sem.idn, 1)
+    ve.tensor_scalar(T.dg[0:W, 0:W], T.ident[0:W, 0:W], mcol(NR - 1), -0.5, AluOpType.mult,
+                     AluOpType.mult).then_inc(sem.dgs, 1)
+    pe.wait_ge(sem.dgs, 1)
     for i in range(NR):
-        pe.matmul(T["ps%d" % i][:, 0:W], T.ones[0:1, 0:D], T.mrow[0:1, 0:W], False, True).then_inc(sem["sb%d" % i], 1)
-    ve.wait_ge(sem.zer, 1)
+        pe.matmul(T["ps%d" % i][:, 0:W], T.on[0:W, 0:D], T.dg[0:W, 0:W], False, True).then_inc(sem["sb%d" % i], 1)
     for i in range(NR):
         ve.wait_ge(sem["sb%d" % i], 1)
-        ve.tensor_tensor(T.pb[:, i * D:i * D + W], T["ps%d" % i][:, 0:W], T.zeros[:, 0:W],
+        ve.tensor_scalar(T.pb[:, i * D:i * D + W], T["ps%d" % i][:, 0:W], 0.0, None,
                          AluOpType.max).then_inc(sem["pp%d" % i], 1)
 
     for i, j in enumerate(order):

@@ -10,11 +10,12 @@ SCRATCH = {
     "kv": ("sbuf", [D, NR * SLOT], "bfloat16"),
     "zb": ("sbuf", [D, D], "bfloat16"),
     "on": ("sbuf", [D, D], "bfloat16"),
-    "zf": ("sbuf", [D, D], "float32"),
+    "zf": ("sbuf", [D, 3 * D], "float32"),
     "cidx": ("sbuf", [D, D], "bfloat16"),
     "ident": ("sbuf", [D, D], "bfloat16"),
+    "negi": ("sbuf", [D, D], "bfloat16"),
     "sc": ("sbuf", [D, NR * D], "float32"),
-    "dg": ("sbuf", [D, D], "bfloat16"),
+    "mb": ("sbuf", [D, 3 * D], "bfloat16"),
     "pb": ("sbuf", [D, NR * D], "bfloat16"),
     "ysb": ("sbuf", [D, D], "bfloat16"),
 }
@@ -22,9 +23,9 @@ for _i in range(NR):
     SCRATCH["pt%d" % _i] = ("psum", [D, 512], "float32")
     SCRATCH["ps%d" % _i] = ("psum", [D, 512], "float32")
 
-SEMAPHORES = (["kld", "vld", "qld", "ms", "cix", "rix", "idn", "sent", "dgs", "yps", "ycp", "sto"]
+SEMAPHORES = (["kld", "vld", "qld", "ms", "cix", "rix", "idn", "ngi", "fil", "stf", "sent", "dgs", "yps", "ycp", "sto"]
               + ["ka%d" % i for i in range(NR)] + ["va%d" % i for i in range(NR)]
-              + ["st%d" % i for i in range(NR)] + ["ru%d" % i for i in range(NR)]
+              + ["st%d" % i for i in range(2)] + ["ru%d" % i for i in range(2)]
               + ["sb%d" % i for i in range(NR)] + ["pp%d" % i for i in range(NR)])
 
 
@@ -88,7 +89,7 @@ def rank_program(g, core, T, topo):
     sc.dma_start(vcol(r), T.v[:, :]).then_inc(sem.vld, 16)
     sy.dma_start(T.qs[:, 0:W], T.q[:, 0:W]).then_inc(sem.qld, 16)
 
-    RI = T.pt3[:, 256:256 + D]
+    RI = T.pt3[:, 0:D]
     ve.memset(T.zb[:, :], 0.0).then_inc(sem.ms, 1)
     ve.memset(T.on[:, :], 1.0).then_inc(sem.ms, 1)
     ve.memset(T.zf[:, :], 0.0).then_inc(sem.ms, 1)
@@ -100,6 +101,8 @@ def rank_program(g, core, T, topo):
     ve.wait_ge(sem.cix, 1)
     ve.wait_ge(sem.rix, 1)
     ve.tensor_tensor(T.ident[:, :], RI, T.cidx[:, :], AluOpType.is_equal).then_inc(sem.idn, 1)
+    ve.wait_ge(sem.idn, 1)
+    ve.tensor_scalar(T.negi[:, :], T.ident[:, :], -0.5, None, AluOpType.mult).then_inc(sem.ngi, 1)
 
     def xfer(dst_core, ap, rsem):
         rid, pid, _se = topo.addr(dst_core)
@@ -137,43 +140,50 @@ def rank_program(g, core, T, topo):
 
     YP = T.pt0[:, 256:256 + W]
 
-    def st_mm(i, j):
-        pe.matmul(T["pt%d" % i][0:W, 0:D], T.qs[:, 0:W], kcol(j), True, True).then_inc(sem["st%d" % i], 1)
+    nf = len(far)
+    assert early == 2 and early + nf == NR and (nf + 1) * D <= 512
+    FT = T.pt2
 
     def s_mm(i, j):
         pe.matmul(T["ps%d" % i][:, 0:W], kcol(j), T.qs[:, 0:W], True, False)
 
     pe.wait_ge(sem.qld, 16)
-    pe.wait_ge(sem.idn, 1)
-    for i, j in enumerate(order):
+    for i, j in enumerate(order[:early]):
         s, n = k_wait(j)
         pe.wait_ge(s, n)
-        st_mm(i, j)
-        if i < early:
-            s_mm(i, j)
-    for i, j in enumerate(order):
-        if i >= early:
-            s_mm(i, j)
+        pe.matmul(T["pt%d" % i][0:W, 0:D], T.qs[:, 0:W], kcol(j), True, True).then_inc(sem["st%d" % i], 1)
+        if i == 0:
+            pe.matmul(FT[0:W, nf * D:(nf + 1) * D], T.qs[:, 0:W], kcol(j), True, True).then_inc(sem.fil, 1)
+        s_mm(i, j)
+    for a, j in enumerate(order[early:]):
+        s, n = k_wait(j)
+        pe.wait_ge(s, n)
+        pe.matmul(FT[0:W, a * D:(a + 1) * D], T.qs[:, 0:W], kcol(j), True, True).then_inc(sem.stf, 1)
+    for a, j in enumerate(order[early:]):
+        s_mm(early + a, j)
 
     def mcol(i):
         return T.sc[0:W, i * D + D - 1:(i + 1) * D]
 
-    for i in range(NR):
+    for i in range(early):
         ve.wait_ge(sem["st%d" % i], 1)
         if i == 0:
             ve.tensor_reduce(mcol(0), T.pt0[0:W, 0:D], AxisListType.X, AluOpType.max).then_inc(sem.ru0, 1)
         else:
             ve.wait_ge(sem["ru%d" % (i - 1)], 1)
-            ve.tensor_tensor_scan(T.sc[0:W, i * D:(i + 1) * D], T["pt%d" % i][0:W, 0:D], T.zf[0:W, :], mcol(i - 1),
+            ve.tensor_tensor_scan(T.sc[0:W, i * D:(i + 1) * D], T["pt%d" % i][0:W, 0:D], T.zf[0:W, 0:D], mcol(i - 1),
                                   AluOpType.max, AluOpType.add).then_inc(sem["ru%d" % i], 1)
+    ve.wait_ge(sem["ru%d" % (early - 1)], 1)
+    ve.wait_ge(sem.fil, 1)
+    ve.wait_ge(sem.stf, nf)
+    ve.tensor_tensor_scan(T.mb[0:W, 0:(nf + 1) * D], FT[0:W, 0:(nf + 1) * D], T.zf[0:W, 0:(nf + 1) * D], mcol(early - 1),
+                          AluOpType.max, AluOpType.add).then_inc(sem.dgs, 1)
 
-    ve.wait_ge(sem["ru%d" % (NR - 1)], 1)
-    ve.wait_ge(sem.idn, 1)
-    ve.tensor_scalar(T.dg[0:W, 0:W], T.ident[0:W, 0:W], mcol(NR - 1), -0.5, AluOpType.mult,
-                     AluOpType.mult).then_inc(sem.dgs, 1)
+    pe.wait_ge(sem.ngi, 1)
     pe.wait_ge(sem.dgs, 1)
     for i in range(NR):
-        pe.matmul(T["ps%d" % i][:, 0:W], T.on[0:W, 0:D], T.dg[0:W, 0:W], False, True).then_inc(sem["sb%d" % i], 1)
+        pe.matmul(T["ps%d" % i][:, 0:W], T.mb[0:W, nf * D:(nf + 1) * D], T.negi[0:W, 0:W], False,
+                  True).then_inc(sem["sb%d" % i], 1)
     for i in range(NR):
         ve.wait_ge(sem["sb%d" % i], 1)
         ve.tensor_scalar(T.pb[:, i * D:i * D + W], T["ps%d" % i][:, 0:W], 0.0, None,

@@ -1,21 +1,23 @@
 from concourse.bass import DstId, RemoteDMATransfer
-from concourse.mybir import AluOpType, AxisListType
+from concourse.mybir import AluOpType, AxisListType, ActivationFunctionType
 
 NR = 4
 D = 128
 SLOT = 2 * D
 
 SCRATCH = {
+    "kd": ("dram", [D, D], "bfloat16"),
     "qs": ("sbuf", [D, D], "bfloat16"),
     "kv": ("sbuf", [D, NR * SLOT], "bfloat16"),
     "zb": ("sbuf", [D, D], "bfloat16"),
     "on": ("sbuf", [D, D], "bfloat16"),
-    "zf": ("sbuf", [D, 3 * D], "float32"),
+    "zf": ("sbuf", [D, 2 * D], "float32"),
+    "zz": ("sbuf", [D, 2 * D], "float32"),
     "cidx": ("sbuf", [D, D], "bfloat16"),
     "ident": ("sbuf", [D, D], "bfloat16"),
     "negi": ("sbuf", [D, D], "bfloat16"),
-    "sc": ("sbuf", [D, NR * D], "float32"),
-    "mb": ("sbuf", [D, 3 * D], "bfloat16"),
+    "sc": ("sbuf", [D, 4], "float32"),
+    "mb": ("sbuf", [D, 2 * D], "bfloat16"),
     "pb": ("sbuf", [D, NR * D], "bfloat16"),
     "ysb": ("sbuf", [D, D], "bfloat16"),
 }
@@ -23,10 +25,11 @@ for _i in range(NR):
     SCRATCH["pt%d" % _i] = ("psum", [D, 512], "float32")
     SCRATCH["ps%d" % _i] = ("psum", [D, 512], "float32")
 
-SEMAPHORES = (["kld", "vld", "qld", "ms", "cix", "rix", "idn", "ngi", "fil", "stf", "sent", "dgs", "yps", "ycp", "sto"]
+SEMAPHORES = (["kst", "kld", "vld", "qld", "ms", "cix", "rix", "idn", "ngi", "fil", "stf", "sent", "dgs", "ycp", "sto",
+               "yp0", "yp1", "st0", "st1", "st2", "ru0", "ru1", "zfl"]
               + ["ka%d" % i for i in range(NR)] + ["va%d" % i for i in range(NR)]
-              + ["st%d" % i for i in range(2)] + ["ru%d" % i for i in range(2)]
-              + ["sb%d" % i for i in range(NR)] + ["pp%d" % i for i in range(NR)])
+              + ["sb%d" % i for i in range(NR)]
+              + ["pp%d%d" % (i, h) for i in range(NR) for h in range(2)])
 
 
 def _bits(mask):
@@ -44,20 +47,17 @@ def _plan(src, cores, topo):
     others = [c for c in cores if c != src]
     far = [c for c in others if topo.chip(c) != topo.chip(src)]
     near = [c for c in others if topo.chip(c) == topo.chip(src)]
-    plan = {}
-    used = []
-    if far:
-        eng = [e for e in _bits(topo.mask(src, far[0])) if all((topo.mask(src, c) >> e) & 1 for c in far)]
-        n = _pow2(len(eng) // len(far))
-        for i, c in enumerate(far):
-            plan[c] = eng[i * n:(i + 1) * n]
-            used += plan[c]
-    if near:
-        eng = [e for e in _bits(topo.mask(src, near[0])) if e not in used]
-        n = _pow2(len(eng) // len(near))
-        for i, c in enumerate(near):
-            plan[c] = eng[i * n:(i + 1) * n]
-    return far, near, plan
+    home = [c for c in cores if topo.chip(c) == topo.chip(src)]
+    s = home.index(src) % len(far)
+    far = far[s:] + far[:s]
+    eng = [e for e in _bits(topo.mask(src, far[0])) if all((topo.mask(src, c) >> e) & 1 for c in far)]
+    leave = eng[:_pow2(len(eng))]
+    nplan = {}
+    eng = [e for e in _bits(topo.mask(src, near[0])) if e not in leave]
+    n = _pow2(len(eng) // len(near))
+    for i, c in enumerate(near):
+        nplan[c] = eng[i * n:(i + 1) * n]
+    return far, near, nplan, leave
 
 
 def _mask(engines):
@@ -72,7 +72,7 @@ def rank_program(g, core, T, topo):
     W = T.tables["WID"][r]
     sem = T.sem
     pe, ve, sy, sc = g.tensor, g.vector, g.sync, g.scalar
-    far, near, plan = _plan(core, cores, topo)
+    far, near, nplan, leave = _plan(core, cores, topo)
     for c in far + near:
         assert topo.may_write(core, c)
 
@@ -82,12 +82,10 @@ def rank_program(g, core, T, topo):
     def vcol(j):
         return T.kv[:, j * SLOT + D:(j + 1) * SLOT]
 
-    def slot(j):
-        return T.kv[:, j * SLOT:(j + 1) * SLOT]
-
+    sy.dma_start(T.kd[:, :], T.k[:, :]).then_inc(sem.kst, 16)
     sy.dma_start(kcol(r), T.k[:, :]).then_inc(sem.kld, 16)
-    sc.dma_start(vcol(r), T.v[:, :]).then_inc(sem.vld, 16)
     sy.dma_start(T.qs[:, 0:W], T.q[:, 0:W]).then_inc(sem.qld, 16)
+    sy.dma_start(vcol(r), T.v[:, :]).then_inc(sem.vld, 16)
 
     RI = T.pt3[:, 0:D]
     ve.memset(T.zb[:, :], 0.0).then_inc(sem.ms, 1)
@@ -104,101 +102,120 @@ def rank_program(g, core, T, topo):
     ve.wait_ge(sem.idn, 1)
     ve.tensor_scalar(T.negi[:, :], T.ident[:, :], -0.5, None, AluOpType.mult).then_inc(sem.ngi, 1)
 
-    def xfer(dst_core, ap, rsem):
+    def xfer(dst_core, engines, src, dst, rsem):
         rid, pid, _se = topo.addr(dst_core)
-        return RemoteDMATransfer(dst_ids=[DstId(rid=rid, pnc=pid)], dma_engine_mask=_mask(plan[dst_core]),
-                                 remote_sem=rsem, src=ap, dst=ap)
+        return RemoteDMATransfer(dst_ids=[DstId(rid=rid, pnc=pid)], dma_engine_mask=_mask(engines),
+                                 remote_sem=rsem, src=src, dst=dst)
 
-    sent = 0
-    g.wait_ge(sem.kld, 16)
-    if far:
-        g.remote_dma_fused([xfer(c, kcol(r), sem["ka%d" % r]) for c in far], local_sem=sem.sent)
-        sent += sum(len(plan[c]) for c in far)
+    assert len(far) == 2 and len(near) == 1
+    first, second = far
+    ka, va = sem["ka%d" % r], sem["va%d" % r]
+    g.wait_ge(sem.kst, 16)
+    g.remote_dma_fused([xfer(first, leave, T.kd[:, :], kcol(r), ka)]
+                       + [xfer(n, nplan[n], T.kd[:, :], kcol(r), ka) for n in near], local_sem=sem.sent)
+    g.remote_dma_fused([xfer(second, leave, T.kd[:, :], kcol(r), ka)], local_sem=sem.sent)
     g.wait_ge(sem.vld, 16)
-    if near:
-        g.remote_dma_fused([xfer(c, slot(r), sem["ka%d" % r]) for c in near], local_sem=sem.sent)
-        sent += sum(len(plan[c]) for c in near)
-    if far:
-        g.remote_dma_fused([xfer(c, vcol(r), sem["va%d" % r]) for c in far], local_sem=sem.sent)
-        sent += sum(len(plan[c]) for c in far)
+    g.remote_dma_fused([xfer(first, leave, vcol(r), vcol(r), va)]
+                       + [xfer(n, nplan[n], vcol(r), vcol(r), va) for n in near], local_sem=sem.sent)
+    g.remote_dma_fused([xfer(second, leave, vcol(r), vcol(r), va)], local_sem=sem.sent)
+    sent = 4 * len(leave) + 2 * sum(len(nplan[n]) for n in near)
 
-    order = [r] + [T.rank_of(c) for c in near] + [T.rank_of(c) for c in far]
     near_ranks = [T.rank_of(c) for c in near]
-    early = 1 + len(near)
+    far_ranks = sorted([T.rank_of(c) for c in far], key=lambda j: _plan(cores[j], cores, topo)[0].index(core))
+    order = [r] + near_ranks + far_ranks
+
+    def count(j):
+        p = _plan(cores[j], cores, topo)
+        return len(p[2][core]) if j in near_ranks else len(p[3])
 
     def k_wait(j):
         if j == r:
             return sem.kld, 16
-        return sem["ka%d" % j], len(_plan(cores[j], cores, topo)[2][core])
+        return sem["ka%d" % j], count(j)
 
     def v_wait(j):
         if j == r:
             return sem.vld, 16
-        if j in near_ranks:
-            return k_wait(j)
-        return sem["va%d" % j], len(_plan(cores[j], cores, topo)[2][core])
+        return sem["va%d" % j], count(j)
 
-    YP = T.pt0[:, 256:256 + W]
+    if W > 64:
+        pieces = [(0, W // 2), (W // 2, W)]
+    else:
+        pieces = [(0, W)]
+    YB = [T.pt0, T.pt1]
+    YP = [YB[h][:, 256:256 + c1 - c0] for h, (c0, c1) in enumerate(pieces)]
 
-    nf = len(far)
-    assert early == 2 and early + nf == NR and (nf + 1) * D <= 512
     FT = T.pt2
+    EB = [T.pt1, T.pt3]
 
     def s_mm(i, j):
         pe.matmul(T["ps%d" % i][:, 0:W], kcol(j), T.qs[:, 0:W], True, False)
 
+    def st_mm(out, j):
+        return pe.matmul(out, T.qs[:, 0:W], kcol(j), True, True)
+
     pe.wait_ge(sem.qld, 16)
-    for i, j in enumerate(order[:early]):
-        s, n = k_wait(j)
-        pe.wait_ge(s, n)
-        pe.matmul(T["pt%d" % i][0:W, 0:D], T.qs[:, 0:W], kcol(j), True, True).then_inc(sem["st%d" % i], 1)
-        if i == 0:
-            pe.matmul(FT[0:W, nf * D:(nf + 1) * D], T.qs[:, 0:W], kcol(j), True, True).then_inc(sem.fil, 1)
-        s_mm(i, j)
-    for a, j in enumerate(order[early:]):
-        s, n = k_wait(j)
-        pe.wait_ge(s, n)
-        pe.matmul(FT[0:W, a * D:(a + 1) * D], T.qs[:, 0:W], kcol(j), True, True).then_inc(sem.stf, 1)
-    for a, j in enumerate(order[early:]):
-        s_mm(early + a, j)
+    pe.wait_ge(*k_wait(r))
+    st_mm(T.pt0[0:W, 0:D], r).then_inc(sem.st0, 1)
+    st_mm(FT[0:W, D:2 * D], r).then_inc(sem.fil, 1)
+    s_mm(0, r)
+    pe.wait_ge(sem.idn, 1)
+    for a, j in enumerate(order[1:3]):
+        pe.wait_ge(*k_wait(j))
+        st_mm(EB[a][0:W, 0:D], j).then_inc(sem["st%d" % (1 + a)], 1)
+    for a, j in enumerate(order[1:3]):
+        s_mm(1 + a, j)
+    pe.wait_ge(*k_wait(order[3]))
+    st_mm(FT[0:W, 0:D], order[3]).then_inc(sem.stf, 1)
+    s_mm(3, order[3])
 
-    def mcol(i):
-        return T.sc[0:W, i * D + D - 1:(i + 1) * D]
-
-    for i in range(early):
-        ve.wait_ge(sem["st%d" % i], 1)
-        if i == 0:
-            ve.tensor_reduce(mcol(0), T.pt0[0:W, 0:D], AxisListType.X, AluOpType.max).then_inc(sem.ru0, 1)
-        else:
-            ve.wait_ge(sem["ru%d" % (i - 1)], 1)
-            ve.tensor_tensor_scan(T.sc[0:W, i * D:(i + 1) * D], T["pt%d" % i][0:W, 0:D], T.zf[0:W, 0:D], mcol(i - 1),
-                                  AluOpType.max, AluOpType.add).then_inc(sem["ru%d" % i], 1)
-    ve.wait_ge(sem["ru%d" % (early - 1)], 1)
+    m0 = T.sc[0:W, 0:1]
+    ve.wait_ge(sem.st0, 1)
+    ve.tensor_reduce(m0, T.pt0[0:W, 0:D], AxisListType.X, AluOpType.max).then_inc(sem.ru0, 1)
+    ve.wait_ge(sem.ru0, 1)
+    ve.tensor_scalar(T.zz[0:W, :], T.zf[0:W, :], m0, None, AluOpType.add).then_inc(sem.zfl, 1)
+    ve.wait_ge(sem.zfl, 1)
+    for a in range(2):
+        ve.wait_ge(sem["st%d" % (1 + a)], 1)
+        ve.tensor_reduce(T.zz[0:W, a:a + 1], EB[a][0:W, 0:D], AxisListType.X, AluOpType.max).then_inc(sem.ru1, 1)
+    ve.wait_ge(sem.ru1, 2)
     ve.wait_ge(sem.fil, 1)
-    ve.wait_ge(sem.stf, nf)
-    ve.tensor_tensor_scan(T.mb[0:W, 0:(nf + 1) * D], FT[0:W, 0:(nf + 1) * D], T.zf[0:W, 0:(nf + 1) * D], mcol(early - 1),
-                          AluOpType.max, AluOpType.add).then_inc(sem.dgs, 1)
+    ve.wait_ge(sem.stf, 1)
+    ve.tensor_tensor_scan(T.mb[0:W, 0:2 * D], FT[0:W, 0:2 * D], T.zz[0:W, 0:2 * D], m0,
+                          AluOpType.max, AluOpType.max).then_inc(sem.dgs, 1)
 
     pe.wait_ge(sem.ngi, 1)
     pe.wait_ge(sem.dgs, 1)
     for i in range(NR):
-        pe.matmul(T["ps%d" % i][:, 0:W], T.mb[0:W, nf * D:(nf + 1) * D], T.negi[0:W, 0:W], False,
+        pe.matmul(T["ps%d" % i][:, 0:W], T.mb[0:W, D:2 * D], T.negi[0:W, 0:W], False,
                   True).then_inc(sem["sb%d" % i], 1)
     for i in range(NR):
-        ve.wait_ge(sem["sb%d" % i], 1)
-        ve.tensor_scalar(T.pb[:, i * D:i * D + W], T["ps%d" % i][:, 0:W], 0.0, None,
-                         AluOpType.max).then_inc(sem["pp%d" % i], 1)
+        q = ve if i % 2 == 0 else sc
+        q.wait_ge(sem["sb%d" % i], 1)
+        for h, (c0, c1) in enumerate(pieces):
+            out, src = T.pb[:, i * D + c0:i * D + c1], T["ps%d" % i][:, c0:c1]
+            if i % 2 == 0:
+                ins = ve.tensor_scalar(out, src, 0.0, None, AluOpType.max)
+            else:
+                ins = sc.activation(out, src, ActivationFunctionType.Relu)
+            ins.then_inc(sem["pp%d%d" % (i, h)], 1)
 
     for i, j in enumerate(order):
-        pe.wait_ge(sem["pp%d" % i], 1)
-        s, n = v_wait(j)
-        pe.wait_ge(s, n)
-        mm = pe.matmul(YP, vcol(j), T.pb[:, i * D:i * D + W], i == 0, i == NR - 1)
-        if i == NR - 1:
-            mm.then_inc(sem.yps, 1)
-    ve.wait_ge(sem.yps, 1)
-    ve.tensor_copy(T.ysb[:, 0:W], YP).then_inc(sem.ycp, 1)
-    sy.wait_ge(sem.ycp, 1)
+        for h, (c0, c1) in enumerate(pieces):
+            pe.wait_ge(sem["pp%d%d" % (i, h)], 1)
+            if h == 0:
+                pe.wait_ge(*v_wait(j))
+            mm = pe.matmul(YP[h], vcol(j), T.pb[:, i * D + c0:i * D + c1], i == 0, i == NR - 1)
+            if i == NR - 1:
+                mm.then_inc(sem["yp%d" % h], 1)
+    for h, (c0, c1) in enumerate(pieces):
+        if h == 0:
+            ve.wait_ge(sem.yp0, 1)
+            ve.tensor_copy(T.ysb[:, c0:c1], YP[h]).then_inc(sem.ycp, 1)
+        else:
+            sc.wait_ge(sem.yp1, 1)
+            sc.activation(T.ysb[:, c0:c1], YP[h], ActivationFunctionType.Copy).then_inc(sem.ycp, 1)
+    sy.wait_ge(sem.ycp, len(pieces))
     sy.dma_start(T.y[:, 0:W], T.ysb[:, 0:W]).then_inc(sem.sto, 16)
     sy.wait_ge(sem.sto, 16)
 

from concourse.bass import DstId, RemoteDMATransfer
from concourse.mybir import AluOpType, AxisListType, ActivationFunctionType

NR = 4
D = 128
SLOT = 2 * D

SCRATCH = {
    "kd": ("dram", [D, D], "bfloat16"),
    "qs": ("sbuf", [D, D], "bfloat16"),
    "kv": ("sbuf", [D, NR * SLOT], "bfloat16"),
    "zb": ("sbuf", [D, D], "bfloat16"),
    "on": ("sbuf", [D, D], "bfloat16"),
    "zf": ("sbuf", [D, 2 * D], "float32"),
    "zz": ("sbuf", [D, 2 * D], "float32"),
    "cidx": ("sbuf", [D, D], "bfloat16"),
    "ident": ("sbuf", [D, D], "bfloat16"),
    "negi": ("sbuf", [D, D], "bfloat16"),
    "sc": ("sbuf", [D, 4], "float32"),
    "mb": ("sbuf", [D, 2 * D], "bfloat16"),
    "pb": ("sbuf", [D, NR * D], "bfloat16"),
    "ysb": ("sbuf", [D, D], "bfloat16"),
}
for _i in range(NR):
    SCRATCH["pt%d" % _i] = ("psum", [D, 512], "float32")
    SCRATCH["ps%d" % _i] = ("psum", [D, 512], "float32")

SEMAPHORES = (["kst", "kld", "vld", "qld", "ms", "cix", "rix", "idn", "ngi", "fil", "stf", "sent", "dgs", "ycp", "sto",
               "yp0", "yp1", "st0", "st1", "st2", "ru0", "ru1", "zfl"]
              + ["ka%d" % i for i in range(NR)] + ["va%d" % i for i in range(NR)]
              + ["sb%d" % i for i in range(NR)]
              + ["pp%d%d" % (i, h) for i in range(NR) for h in range(2)])


def _bits(mask):
    return [e for e in range(mask.bit_length()) if (mask >> e) & 1]


def _pow2(n):
    p = 1
    while p * 2 <= n:
        p *= 2
    return p


def _plan(src, cores, topo):
    others = [c for c in cores if c != src]
    far = [c for c in others if topo.chip(c) != topo.chip(src)]
    near = [c for c in others if topo.chip(c) == topo.chip(src)]
    home = [c for c in cores if topo.chip(c) == topo.chip(src)]
    s = home.index(src) % len(far)
    far = far[s:] + far[:s]
    eng = [e for e in _bits(topo.mask(src, far[0])) if all((topo.mask(src, c) >> e) & 1 for c in far)]
    leave = eng[:_pow2(len(eng))]
    nplan = {}
    eng = [e for e in _bits(topo.mask(src, near[0])) if e not in leave]
    n = _pow2(len(eng) // len(near))
    for i, c in enumerate(near):
        nplan[c] = eng[i * n:(i + 1) * n]
    return far, near, nplan, leave


def _mask(engines):
    return sum(1 << e for e in engines)


def rank_program(g, core, T, topo):
    r = T.rank_of(core)
    if r is None:
        return
    cores = list(T.cores)
    W = T.tables["WID"][r]
    sem = T.sem
    pe, ve, sy, sc = g.tensor, g.vector, g.sync, g.scalar
    far, near, nplan, leave = _plan(core, cores, topo)
    for c in far + near:
        assert topo.may_write(core, c)

    def kcol(j):
        return T.kv[:, j * SLOT:j * SLOT + D]

    def vcol(j):
        return T.kv[:, j * SLOT + D:(j + 1) * SLOT]

    sy.dma_start(T.kd[:, :], T.k[:, :]).then_inc(sem.kst, 16)
    sy.dma_start(kcol(r), T.k[:, :]).then_inc(sem.kld, 16)
    sy.dma_start(T.qs[:, 0:W], T.q[:, 0:W]).then_inc(sem.qld, 16)
    sy.dma_start(vcol(r), T.v[:, :]).then_inc(sem.vld, 16)

    RI = T.pt3[:, 0:D]
    ve.memset(T.zb[:, :], 0.0).then_inc(sem.ms, 1)
    ve.memset(T.on[:, :], 1.0).then_inc(sem.ms, 1)
    ve.memset(T.zf[:, :], 0.0).then_inc(sem.ms, 1)
    ve.wait_ge(sem.ms, 3)
    ve.tensor_tensor_scan(T.cidx[:, :], T.zb[:, :], T.on[:, :], 0.0, AluOpType.add, AluOpType.add).then_inc(sem.cix, 1)
    pe.wait_ge(sem.ms, 3)
    pe.wait_ge(sem.cix, 1)
    pe.matmul(RI, T.cidx[0:1, :], T.on[0:1, :], True, True).then_inc(sem.rix, 1)
    ve.wait_ge(sem.cix, 1)
    ve.wait_ge(sem.rix, 1)
    ve.tensor_tensor(T.ident[:, :], RI, T.cidx[:, :], AluOpType.is_equal).then_inc(sem.idn, 1)
    ve.wait_ge(sem.idn, 1)
    ve.tensor_scalar(T.negi[:, :], T.ident[:, :], -0.5, None, AluOpType.mult).then_inc(sem.ngi, 1)

    def xfer(dst_core, engines, src, dst, rsem):
        rid, pid, _se = topo.addr(dst_core)
        return RemoteDMATransfer(dst_ids=[DstId(rid=rid, pnc=pid)], dma_engine_mask=_mask(engines),
                                 remote_sem=rsem, src=src, dst=dst)

    assert len(far) == 2 and len(near) == 1
    first, second = far
    ka, va = sem["ka%d" % r], sem["va%d" % r]
    g.wait_ge(sem.kst, 16)
    g.remote_dma_fused([xfer(first, leave, T.kd[:, :], kcol(r), ka)]
                       + [xfer(n, nplan[n], T.kd[:, :], kcol(r), ka) for n in near], local_sem=sem.sent)
    g.remote_dma_fused([xfer(second, leave, T.kd[:, :], kcol(r), ka)], local_sem=sem.sent)
    g.wait_ge(sem.vld, 16)
    g.remote_dma_fused([xfer(first, leave, vcol(r), vcol(r), va)]
                       + [xfer(n, nplan[n], vcol(r), vcol(r), va) for n in near], local_sem=sem.sent)
    g.remote_dma_fused([xfer(second, leave, vcol(r), vcol(r), va)], local_sem=sem.sent)
    sent = 4 * len(leave) + 2 * sum(len(nplan[n]) for n in near)

    near_ranks = [T.rank_of(c) for c in near]
    far_ranks = sorted([T.rank_of(c) for c in far], key=lambda j: _plan(cores[j], cores, topo)[0].index(core))
    order = [r] + near_ranks + far_ranks

    def count(j):
        p = _plan(cores[j], cores, topo)
        return len(p[2][core]) if j in near_ranks else len(p[3])

    def k_wait(j):
        if j == r:
            return sem.kld, 16
        return sem["ka%d" % j], count(j)

    def v_wait(j):
        if j == r:
            return sem.vld, 16
        return sem["va%d" % j], count(j)

    if W > 64:
        pieces = [(0, W // 2), (W // 2, W)]
    else:
        pieces = [(0, W)]
    YB = [T.pt0, T.pt1]
    YP = [YB[h][:, 256:256 + c1 - c0] for h, (c0, c1) in enumerate(pieces)]

    FT = T.pt2
    EB = [T.pt1, T.pt3]

    def s_mm(i, j):
        pe.matmul(T["ps%d" % i][:, 0:W], kcol(j), T.qs[:, 0:W], True, False)

    def st_mm(out, j):
        return pe.matmul(out, T.qs[:, 0:W], kcol(j), True, True)

    pe.wait_ge(sem.qld, 16)
    pe.wait_ge(*k_wait(r))
    st_mm(T.pt0[0:W, 0:D], r).then_inc(sem.st0, 1)
    st_mm(FT[0:W, D:2 * D], r).then_inc(sem.fil, 1)
    s_mm(0, r)
    pe.wait_ge(sem.idn, 1)
    for a, j in enumerate(order[1:3]):
        pe.wait_ge(*k_wait(j))
        st_mm(EB[a][0:W, 0:D], j).then_inc(sem["st%d" % (1 + a)], 1)
    for a, j in enumerate(order[1:3]):
        s_mm(1 + a, j)
    pe.wait_ge(*k_wait(order[3]))
    st_mm(FT[0:W, 0:D], order[3]).then_inc(sem.stf, 1)
    s_mm(3, order[3])

    m0 = T.sc[0:W, 0:1]
    ve.wait_ge(sem.st0, 1)
    ve.tensor_reduce(m0, T.pt0[0:W, 0:D], AxisListType.X, AluOpType.max).then_inc(sem.ru0, 1)
    ve.wait_ge(sem.ru0, 1)
    ve.tensor_scalar(T.zz[0:W, :], T.zf[0:W, :], m0, None, AluOpType.add).then_inc(sem.zfl, 1)
    ve.wait_ge(sem.zfl, 1)
    for a in range(2):
        ve.wait_ge(sem["st%d" % (1 + a)], 1)
        ve.tensor_reduce(T.zz[0:W, a:a + 1], EB[a][0:W, 0:D], AxisListType.X, AluOpType.max).then_inc(sem.ru1, 1)
    ve.wait_ge(sem.ru1, 2)
    ve.wait_ge(sem.fil, 1)
    ve.wait_ge(sem.stf, 1)
    ve.tensor_tensor_scan(T.mb[0:W, 0:2 * D], FT[0:W, 0:2 * D], T.zz[0:W, 0:2 * D], m0,
                          AluOpType.max, AluOpType.max).then_inc(sem.dgs, 1)

    pe.wait_ge(sem.ngi, 1)
    pe.wait_ge(sem.dgs, 1)
    for i in range(NR):
        pe.matmul(T["ps%d" % i][:, 0:W], T.mb[0:W, D:2 * D], T.negi[0:W, 0:W], False,
                  True).then_inc(sem["sb%d" % i], 1)
    for i in range(NR):
        q = ve if i % 2 == 0 else sc
        q.wait_ge(sem["sb%d" % i], 1)
        for h, (c0, c1) in enumerate(pieces):
            out, src = T.pb[:, i * D + c0:i * D + c1], T["ps%d" % i][:, c0:c1]
            if i % 2 == 0:
                ins = ve.tensor_scalar(out, src, 0.0, None, AluOpType.max)
            else:
                ins = sc.activation(out, src, ActivationFunctionType.Relu)
            ins.then_inc(sem["pp%d%d" % (i, h)], 1)

    for i, j in enumerate(order):
        for h, (c0, c1) in enumerate(pieces):
            pe.wait_ge(sem["pp%d%d" % (i, h)], 1)
            if h == 0:
                pe.wait_ge(*v_wait(j))
            mm = pe.matmul(YP[h], vcol(j), T.pb[:, i * D + c0:i * D + c1], i == 0, i == NR - 1)
            if i == NR - 1:
                mm.then_inc(sem["yp%d" % h], 1)
    for h, (c0, c1) in enumerate(pieces):
        if h == 0:
            ve.wait_ge(sem.yp0, 1)
            ve.tensor_copy(T.ysb[:, c0:c1], YP[h]).then_inc(sem.ycp, 1)
        else:
            sc.wait_ge(sem.yp1, 1)
            sc.activation(T.ysb[:, c0:c1], YP[h], ActivationFunctionType.Copy).then_inc(sem.ycp, 1)
    sy.wait_ge(sem.ycp, len(pieces))
    sy.dma_start(T.y[:, 0:W], T.ysb[:, 0:W]).then_inc(sem.sto, 16)
    sy.wait_ge(sem.sto, 16)

    g.wait_ge(sem.sent, sent)
